import numpy as np
import ml_dtypes


def mxq(x, axis, fmt="e4m3"):
    dtype, down = {"e4m3": (ml_dtypes.float8_e4m3fn, 7), "e5m2": (ml_dtypes.float8_e5m2, 14)}[fmt]
    v = np.moveaxis(np.asarray(x, np.float32).astype(ml_dtypes.bfloat16).astype(np.float64), axis, -1)
    blocks = v.reshape(v.shape[:-1] + (-1, 32))
    amax = np.abs(blocks).max(-1, keepdims=True)
    byte = np.maximum(np.where(amax > 0, np.frexp(amax)[1] - 1 + 127, 0) - down, 1)
    scale = np.exp2(byte - 127.0)
    codes = (blocks / scale).astype(np.float32).astype(dtype).astype(np.float64)
    return np.moveaxis((codes * scale).reshape(v.shape), -1, axis)


WIDE = False


def mx_kscale(k):
    if not WIDE:
        return np.ones(k)
    levels = np.array([10, -10, 5, -5, 0])
    if k % 512:
        return np.exp2(np.random.permutation(np.resize(levels, k // 32))).repeat(32)
    a = np.empty((k // 512, 16))
    for p in range(k // 512):
        a[p, :8] = np.random.permutation(np.resize(levels, 8))
        for g in range(8):
            far = levels[np.abs(levels - a[p, g]) >= 10]
            a[p, g + 8] = far[np.random.randint(len(far))]
    return np.exp2(a.ravel()).repeat(32)


def f64(x):
    return np.asarray(x).astype(np.float64)


def striped(idx):
    return np.tile(idx.reshape(-1, 16).T, (8, 1)).astype(np.uint16)


def unstriped(offs):
    return offs[:16].T.reshape(-1).astype(np.int64)


E2M1 = np.array([0.0, 0.5, 1.0, 1.5, 2.0, 3.0, 4.0, 6.0, -0.0, -0.5, -1.0, -1.5, -2.0, -3.0, -4.0, -6.0])


def pack_weight(w, fmt):
    k, n = w.shape
    w = f64(np.asarray(w, np.float32).astype(ml_dtypes.bfloat16)).reshape(k // 32, 32, n)
    amax = np.abs(w).max(1)
    if fmt == "e4m3":
        byte = np.frexp(amax)[1] - 1 + 127 - 7
    else:
        mant, ex = np.frexp(amax / 6.0)
        byte = np.where(mant > 0.5, ex, ex - 1) + 127
    byte = np.clip(np.where(amax > 0, byte, 1), 1, 254)
    scaled = (w * np.exp2(127.0 - byte)[:, None, :]).reshape(k, n).astype(np.float32)
    by_word = np.ascontiguousarray(scaled.reshape(k // 512, 128, 4, n).transpose(0, 1, 3, 2))
    if fmt == "e4m3":
        words = by_word.astype(ml_dtypes.float8_e4m3fn).view(np.uint8)
    else:
        c = by_word.astype(ml_dtypes.float4_e2m1fn).view(np.uint8) & 0xF
        words = (c[..., 0::2] | (c[..., 1::2] << 4)).reshape(k // 512, 128, 2 * n)
    return np.ascontiguousarray(words), np.ascontiguousarray(byte.astype(np.uint8).reshape(k // 512, 16, n))


def unpack_weight(words, scales, fmt):
    g, _, n = scales.shape
    words = np.ascontiguousarray(words).reshape(g, 128, n, -1)
    if fmt == "e4m3":
        vals = words.view(ml_dtypes.float8_e4m3fn).astype(np.float64)
    else:
        nib = np.empty((g, 128, n, 4), np.uint8)
        nib[..., 0::2] = words & 0xF
        nib[..., 1::2] = words >> 4
        vals = E2M1[nib]
    vals = vals * np.repeat(np.exp2(scales.astype(np.float64) - 127.0), 8, axis=1)[..., None]
    return vals.transpose(0, 1, 3, 2).reshape(g * 512, n)


def gelu(v):
    return 0.5 * v * (1.0 + np.tanh(np.sqrt(2.0 / np.pi) * (v + 0.044715 * v**3)))


K, T, E, C, H, N = 1024, 640, 5, 256, 512, 512


def by_expert(wq, xq):
    return np.concatenate([wq[e].T @ xq[:, e * C:(e + 1) * C] for e in range(E)], axis=1)


def setup_inputs():
    n = np.random.standard_normal
    s = mx_kscale(K)
    u = mx_kscale(H)
    first = np.random.permutation(np.repeat(np.arange(E), T // E))
    second = (first + 1 + np.random.permutation(np.repeat(np.arange(E - 1), -(-T // (E - 1)))[:T])) % E
    while np.bincount(second, minlength=E).max() != T // E:
        load = np.bincount(second, minlength=E); hi, lo = int(load.argmax()), int(load.argmin())
        t = np.flatnonzero((second == hi) & (first != lo))[0]; second[t] = lo
    slot_token = np.empty(E * C, np.int64); pos = np.empty((2, T), np.int64); fill = np.zeros(E, np.int64)
    place = np.stack([np.random.permutation(C) for _ in range(E)])
    for r, deal in enumerate((first, second)):
        for t in np.random.permutation(T):
            e = deal[t]; j = e * C + place[e, fill[e]]; fill[e] += 1; slot_token[j] = t; pos[r, t] = j
    g = np.random.uniform(0.2, 0.8, T)
    x = pack_weight(n((K, T)) * s[:, None], "e4m3")
    return {
        "x_words": x[0],
        "x_scales": x[1],
        "w1": (n((E, K, H)) / np.sqrt(K) / s[None, :, None] * u).astype(np.float32),
        "w2": (n((H, N)) / np.sqrt(H) / u[:, None]).astype(np.float32),
        "gate": np.stack([np.tile(g, (128, 1)), np.tile(1.0 - g, (128, 1))]).astype(np.float32),
        "offs": striped(slot_token),
        "pos1": striped(pos[0]),
        "pos2": striped(pos[1]),
    }


def reference(x_words, x_scales, w1, w2, gate, offs, pos1, pos2):
    w1q = mxq(f64(w1), 1, "e4m3")
    w2q = mxq(f64(w2), 0, "e4m3")
    idx = unstriped(offs)
    xq = unpack_weight(x_words, x_scales, "e4m3")[:, idx]
    h = gelu(by_expert(w1q, xq))
    c = sum(f64(gate[r, :1]) * h[:, unstriped(p)] for r, p in enumerate((pos1, pos2)))
    return w2q.T @ mxq(c, 0, "e4m3")

@@ -1,0 +1,215 @@
+from contextlib import ExitStack
+
+import concourse.mybir as mybir
+from concourse.masks import make_identity
+
+K, T, E, C, H, N = 1024, 640, 5, 256, 512, 512
+S = E * C
+FLOPS = 2 * K * H * S + 2 * H * N * T
+
+F32 = mybir.dt.float32
+BF16 = mybir.dt.bfloat16
+I32 = mybir.dt.int32
+U32 = mybir.dt.uint32
+U16 = mybir.dt.uint16
+U8 = mybir.dt.uint8
+FP8X4 = mybir.dt.float8_e4m3fn_x4
+MULT = mybir.AluOpType.mult
+GELU = mybir.ActivationFunctionType.Gelu_apprx_tanh
+
+P = 128
+PACK = 4
+PASSES = K // (P * PACK)
+BLOCKS = H // P
+TILES = T // P
+
+
+def tile_moe_sdn_lin_gelu_kernel(tc, x_words, x_scales, w1, w2, gate, offs, pos1, pos2, out):
+    nc = tc.nc
+    with ExitStack() as ctx:
+        keep = ctx.enter_context(tc.tile_pool(name="keep", bufs=1))
+        mxp = ctx.enter_context(tc.psum_pool(name="mxp", bufs=4))
+        trp = ctx.enter_context(tc.psum_pool(name="trp", bufs=4))
+        share = {"gw1_2": "grp3", "gw1_3": "grp5", "h0": "raw5", "h1": "raw4", "ct": "raw13", "h2": "raw15", "h3": "raw14", "prod1_1": "grp15", "prod1_0": "grp11", "prod2_0": "grp23", "prod2_1": "grp8", "grp24": "raw22", "stage0_0": "raw0", "stage0_1": "raw1", "stage2_0": "raw2", "stage2_1": "raw3", "stage4_0": "raw8", "stage1_0": "raw1", "stage3_0": "raw3", "grp20": "grp6", "grp21": "grp7", "grp22": "grp8", "grp16": "grp0", "grp17": "grp1", "grp18": "grp2", "grp19": "grp4"}
+        made = {}
+
+        def sb(name, shape=None, dtype=None):
+            if name not in made:
+                made[name] = keep.tile(shape, dtype, name=name, tag=share.get(name, name), align_bytes=64)
+            return made[name]
+
+        offs_t = keep.tile([P, S // 16], U16, name="offs_t")
+        pos_t = [keep.tile([P, T // 16], U16, name="pos_t%d" % r) for r in range(2)]
+        xw = [keep.tile([P, T], I32, name="xw%d" % s) for s in range(PASSES)]
+        xs = keep.tile([P, T], U8, name="xs")
+        gate_t = [keep.tile([P, T], F32, name="gate_t%d" % r) for r in range(2)]
+        ident = keep.tile([P, P], F32, name="ident")
+        warm = keep.tile([P, 8], F32, name="warm")
+        warm2 = keep.tile([P, 8], F32, name="warm2")
+
+        nc.vector.memset(xs[:].bitcast(I32), 0)
+        nc.gpsimd.memset(warm[:], 0.0)
+        nc.scalar.activation(warm2[:], warm[:], GELU)
+        make_identity(nc, ident[:])
+
+        chunks = [(e, s, 0, 256) for e in range(E) for s in range(PASSES)] + [(e, s, 256, 256) for e in range(3) for s in range(PASSES)] + [(e, s, c0, 128) for c0 in (256, 384) for e in range(3, E) for s in range(PASSES)]
+        W2 = len(chunks)
+
+        def load(what):
+            if what == "offs":
+                nc.sync.dma_start(offs_t[:], offs)
+            elif what == "pos":
+                nc.sync.dma_start(pos_t[0][:], pos1)
+                nc.sync.dma_start(pos_t[1][:], pos2)
+            elif what in ("x0", "x1"):
+                s = 0 if what == "x0" else 1
+                nc.sync.dma_start(out=xw[s][:], in_=x_words[s].rearrange("p t d -> p (t d)").bitcast(I32))
+            elif what == "xs":
+                for q in range(4):
+                    nc.sync.dma_start(out=xs[32 * q:32 * q + 8, :].bitcast(I32), in_=x_scales[:, 4 * q:4 * q + 4, :].bitcast(I32))
+            elif what == "gate":
+                for r in range(2):
+                    nc.sync.dma_start(out=gate_t[r][:], in_=gate[r])
+            else:
+                if what == W2:
+                    rows = w2
+                else:
+                    e, s, c0, width = chunks[what]
+                    rows = w1[e, s * 512:(s + 1) * 512, c0:c0 + width]
+                raw = sb("raw%d" % what, [P, PACK, rows.shape[1]], F32)
+                nc.sync.dma_start(out=raw[:], in_=rows.rearrange("(p j) w -> p j w", j=PACK))
+
+        def cast(i, engine):
+            raw = sb("raw%d" % i)
+            grouped = sb("grp%d" % i, [P, raw.shape[2] * PACK], BF16)
+            dst = grouped[:].rearrange("p (c i t) -> p c t i", i=4, t=PACK)
+            src = raw[:].rearrange("p t (c i) -> p c t i", i=4)
+            if engine == "v":
+                nc.vector.tensor_copy(out=dst, in_=src)
+            elif engine == "g":
+                nc.gpsimd.tensor_copy(out=dst, in_=src)
+            else:
+                nc.scalar.copy(out=dst, in_=src)
+
+        def quantise(i):
+            width = sb("raw%d" % i).shape[2]
+            codes = sb("codes%d" % i, [P, width], U32)
+            scales = sb("scales%d" % i, [P, width], U8)
+            nc.vector.quantize_mx(out=codes[:].bitcast(FP8X4), scales=scales[:], in_=sb("grp%d" % i)[:])
+
+        def gather_tokens(e):
+            lst = offs_t[:, e * C // 16:(e + 1) * C // 16]
+            nc.vector.tensor_copy(sb("gw0_%d" % e, [P, C], U32)[:], xw[0][:].bitcast(U32).indirect(lst))
+            nc.vector.tensor_copy(sb("gw1_%d" % e, [P, C], U32)[:], xw[1][:].bitcast(U32).indirect(lst))
+            nc.vector.tensor_copy(sb("gs_%d" % e, [P, C], U8)[:], xs[:].indirect(lst))
+
+        def first_layer(i, only=None):
+            e, s, c0, width = chunks[i]
+            cols = slice(e * C, (e + 1) * C)
+            for b0 in range(0, width, P):
+                if only is not None and b0 != only * P:
+                    continue
+                acc = mxp.tile([P, C], F32, name="acc", tag="mx")
+                for s in range(PASSES):
+                    nc.tensor.matmul_mx(
+                        out=acc[:], lhsT=sb("codes%d" % (i + s))[:, b0:b0 + P].bitcast(FP8X4),
+                        lhsT_scale=sb("scales%d" % (i + s))[:, b0:b0 + P],
+                        rhs=sb("gw%d_%d" % (s, e))[:].bitcast(FP8X4), rhs_scale=sb("gs_%d" % e)[4 * s:P, :],
+                        start=(s == 0), stop=(s == PASSES - 1))
+                nc.scalar.activation(sb("h%d" % ((c0 + b0) // P), [P, S], F32)[:, cols], acc[:], GELU)
+
+        def products(b, r, i0, i1):
+            toks = slice(i0 * P, i1 * P)
+            prod = sb("prod%d_%d" % (b, r), [P, T], F32)
+            nc.vector.tensor_tensor(prod[:, toks], sb("h%d" % b)[:].indirect(pos_t[r][:, i0 * 8:i1 * 8]), gate_t[r][:, toks], MULT)
+
+        def sums(b, i0, i1):
+            ct4 = sb("ct", [P, TILES * H], BF16)[:].rearrange("p (i u q e) -> p i u q e", i=TILES, u=2, e=2)
+            acc = trp.tile([P, i1 - i0, P], F32, name="sums", tag="tr")
+            for i in range(i0, i1):
+                for r in range(2):
+                    nc.tensor.matmul(acc[:, i - i0, :], lhsT=sb("prod%d_%d" % (b, r))[:, i * P:(i + 1) * P], rhs=ident[:],
+                                     is_transpose=True, start=(r == 0), stop=(r == 1))
+            nc.scalar.copy(out=ct4[:, i0:i1, :, 32 * b:32 * (b + 1), :],
+                           in_=acc[:].rearrange("p i (m u e) -> p i u m e", u=2, e=2))
+
+        out_v = out.rearrange("(nb p) t -> p nb t", p=P)
+
+        def turn(i0, i1):
+            n = i1 - i0
+            xt = trp.tile([P, n, 2, P], F32, name="xt", tag="tr")
+            for i in range(i0, i1):
+                words = sb("ct")[:, i * H:(i + 1) * H].bitcast(F32)
+                for u in range(2):
+                    nc.tensor.transpose(xt[:, i - i0, u, :], words[:, u * P:(u + 1) * P], ident[:])
+            cg = sb("cg%d" % i0, [P, n * P * PACK], BF16)
+            nc.scalar.copy(out=cg[:].bitcast(F32).rearrange("p (i r u) -> p i r u", u=2, i=n), in_=xt[:].rearrange("p i u r -> p i r u"))
+
+        def quant_c(i0, i1):
+            n = i1 - i0
+            cc = sb("cc%d" % i0, [P, n * P], U32)
+            cs = sb("cs%d" % i0, [P, n * P], U8)
+            nc.vector.quantize_mx(out=cc[:].bitcast(FP8X4), scales=cs[:], in_=sb("cg%d" % i0)[:])
+
+        def second(i0, i1, engines):
+            n = i1 - i0
+            per = N // P // n
+            w2c, w2s = sb("codes%d" % W2), sb("scales%d" % W2)
+            for part in range(n):
+                res = mxp.tile([P, per, n * P], F32, name="res", tag="mx")
+                for j in range(per):
+                    nb = part * per + j
+                    nc.tensor.matmul_mx(
+                        out=res[:, j, :], lhsT=w2c[:, nb * P:(nb + 1) * P].bitcast(FP8X4), lhsT_scale=w2s[:, nb * P:(nb + 1) * P],
+                        rhs=sb("cc%d" % i0)[:].bitcast(FP8X4), rhs_scale=sb("cs%d" % i0)[:], start=True, stop=True)
+                stage = sb("stage%d_%d" % (i0, part), [P, per, n * P], F32)
+                if engines[part] == "v":
+                    nc.vector.tensor_copy(out=stage[:], in_=res[:])
+                else:
+                    nc.scalar.copy(out=stage[:], in_=res[:])
+                nc.sync.dma_start(out=out_v[:, part * per:(part + 1) * per, i0 * P:i1 * P], in_=stage[:])
+
+        for what in ["offs", "x0", 0, "xs", 1, "x1", 2, 3, 4, 5, 6, 7, "pos", 8, 9, 10, "gate"] + list(range(11, 25)):
+            load(what)
+        for e in range(E):
+            if e < 2:
+                gather_tokens(e)
+        for i in range(10):
+            cast(i, "v" if i in (7, 9) else "s")
+            quantise(i)
+            if i in (3, 5, 6):
+                gather_tokens({3: 2, 5: 3, 6: 4}[i])
+        for i in range(0, 10, 2):
+            first_layer(i)
+        for i in range(10, 14):
+            cast(i, "s")
+            quantise(i)
+        products(0, 0, 0, 5)
+        products(0, 1, 0, 5)
+        products(1, 0, 0, 5)
+        for i in range(14, 16):
+            cast(i, "s")
+            quantise(i)
+        products(1, 1, 0, 5)
+        for i in range(16, 24):
+            cast(i, "s" if i in (17, 19) else "v")
+            quantise(i)
+        for i in range(10, 24, 2):
+            first_layer(i)
+        for b in range(2):
+            sums(b, 0, 3)
+            sums(b, 3, 5)
+        products(2, 0, 0, 5)
+        products(2, 1, 0, 5)
+        sums(2, 0, 3)
+        sums(2, 3, 5)
+        cast(24, "s")
+        quantise(24)
+        groups = ((0, 2, "sv"), (2, 4, "sv"), (4, 5, "v"))
+        for i0, i1, eng in groups:
+            products(3, 0, i0, i1)
+            products(3, 1, i0, i1)
+            sums(3, i0, i1)
+            turn(i0, i1)
+            quant_c(i0, i1)
+            second(i0, i1, eng)

@@ -29,9 +29,10 @@ def tile_moe_sdn_lin_gelu_kernel(tc, x_words, x_scales, w1, w2, gate, offs, pos1
     with ExitStack() as ctx:
         keep = ctx.enter_context(tc.tile_pool(name="keep", bufs=1))
         mxp = ctx.enter_context(tc.psum_pool(name="mxp", bufs=4))
-        trp = ctx.enter_context(tc.psum_pool(name="trp", bufs=4))
-        share = {"gw1_2": "grp3", "gw1_3": "grp5", "h0": "raw5", "h1": "raw4", "ct": "raw13", "h2": "raw15", "h3": "raw14", "prod1_1": "grp15", "prod1_0": "grp11", "prod2_0": "grp23", "prod2_1": "grp8", "grp24": "raw22", "stage0_0": "raw0", "stage0_1": "raw1", "stage2_0": "raw2", "stage2_1": "raw3", "stage4_0": "raw8", "stage1_0": "raw1", "stage3_0": "raw3", "grp20": "grp6", "grp21": "grp7", "grp22": "grp8", "grp16": "grp0", "grp17": "grp1", "grp18": "grp2", "grp19": "grp4"}
+        trp = ctx.enter_context(tc.psum_pool(name="trp", bufs=1))
+        share = {"ct": "raw23", "h2": "raw19", "h3": "raw22", "prod1_0": "grp13", "prod1_1": "grp4", "prod2_1": "grp23", "grp24": "raw21", "grp25": "raw22", "gw1_2": "grp3", "gw1_3": "grp5", "h0": "raw5", "h1": "raw4", "stage0_0": "raw0", "stage0_1": "raw1", "stage2_0": "raw2", "stage2_1": "raw3", "stage4_0": "raw8", "stage4_1": "raw6", "grp20": "grp6", "grp21": "grp7", "grp22": "grp8", "grp16": "grp0", "grp17": "grp1", "grp18": "grp2", "grp19": "grp4"}
         made = {}
+        where = {}
 
         def sb(name, shape=None, dtype=None):
             if name not in made:
@@ -67,12 +68,12 @@ def tile_moe_sdn_lin_gelu_kernel(tc, x_words, x_scales, w1, w2, gate, offs, pos1
             elif what == "xs":
                 for q in range(4):
                     nc.sync.dma_start(out=xs[32 * q:32 * q + 8, :].bitcast(I32), in_=x_scales[:, 4 * q:4 * q + 4, :].bitcast(I32))
-            elif what == "gate":
-                for r in range(2):
-                    nc.sync.dma_start(out=gate_t[r][:], in_=gate[r])
+            elif what in ("g0", "g1"):
+                r = 0 if what == "g0" else 1
+                nc.sync.dma_start(out=gate_t[r][:], in_=gate[r])
             else:
-                if what == W2:
-                    rows = w2
+                if what >= W2:
+                    rows = w2[:, (what - W2) * 256:(what - W2 + 1) * 256]
                 else:
                     e, s, c0, width = chunks[what]
                     rows = w1[e, s * 512:(s + 1) * 512, c0:c0 + width]
@@ -107,7 +108,7 @@ def tile_moe_sdn_lin_gelu_kernel(tc, x_words, x_scales, w1, w2, gate, offs, pos1
             e, s, c0, width = chunks[i]
             cols = slice(e * C, (e + 1) * C)
             for b0 in range(0, width, P):
-                if only is not None and b0 != only * P:
+                if only is not None and b0 // P not in only:
                     continue
                 acc = mxp.tile([P, C], F32, name="acc", tag="mx")
                 for s in range(PASSES):
@@ -120,24 +121,29 @@ def tile_moe_sdn_lin_gelu_kernel(tc, x_words, x_scales, w1, w2, gate, offs, pos1
 
         def products(b, r, i0, i1):
             toks = slice(i0 * P, i1 * P)
-            prod = sb("prod%d_%d" % (b, r), [P, T], F32)
-            nc.vector.tensor_tensor(prod[:, toks], sb("h%d" % b)[:].indirect(pos_t[r][:, i0 * 8:i1 * 8]), gate_t[r][:, toks], MULT)
+            if b < 3:
+                prod = sb("prod%d_%d" % (b, r), [P, T], F32)[:, toks]
+            else:
+                prod = sb("prodg%d" % i0, [P, 2, (i1 - i0) * P], F32)[:, r, :]
+            for i in range(i0, i1):
+                where[(b, r, i)] = prod[:, (i - i0) * P:(i - i0 + 1) * P]
+            nc.vector.tensor_tensor(prod, sb("h%d" % b)[:].indirect(pos_t[r][:, i0 * 8:i1 * 8]), gate_t[r][:, toks], MULT)
 
-        def sums(b, i0, i1):
+        def sums(b, i0, i1, tag):
             ct4 = sb("ct", [P, TILES * H], BF16)[:].rearrange("p (i u q e) -> p i u q e", i=TILES, u=2, e=2)
-            acc = trp.tile([P, i1 - i0, P], F32, name="sums", tag="tr")
+            acc = trp.tile([P, i1 - i0, P], F32, name="sums", tag=tag)
             for i in range(i0, i1):
                 for r in range(2):
-                    nc.tensor.matmul(acc[:, i - i0, :], lhsT=sb("prod%d_%d" % (b, r))[:, i * P:(i + 1) * P], rhs=ident[:],
+                    nc.tensor.matmul(acc[:, i - i0, :], lhsT=where[(b, r, i)], rhs=ident[:],
                                      is_transpose=True, start=(r == 0), stop=(r == 1))
             nc.scalar.copy(out=ct4[:, i0:i1, :, 32 * b:32 * (b + 1), :],
                            in_=acc[:].rearrange("p i (m u e) -> p i u m e", u=2, e=2))
 
         out_v = out.rearrange("(nb p) t -> p nb t", p=P)
 
-        def turn(i0, i1):
+        def turn(i0, i1, tag):
             n = i1 - i0
-            xt = trp.tile([P, n, 2, P], F32, name="xt", tag="tr")
+            xt = trp.tile([P, n, 2, P], F32, name="xt", tag=tag)
             for i in range(i0, i1):
                 words = sb("ct")[:, i * H:(i + 1) * H].bitcast(F32)
                 for u in range(2):
@@ -153,12 +159,14 @@ def tile_moe_sdn_lin_gelu_kernel(tc, x_words, x_scales, w1, w2, gate, offs, pos1
 
         def second(i0, i1, engines):
             n = i1 - i0
-            per = N // P // n
-            w2c, w2s = sb("codes%d" % W2), sb("scales%d" % W2)
-            for part in range(n):
+            n_parts = len(engines)
+            per = N // P // n_parts
+            for part in range(n_parts):
                 res = mxp.tile([P, per, n * P], F32, name="res", tag="mx")
                 for j in range(per):
                     nb = part * per + j
+                    w2c, w2s = sb("codes%d" % (W2 + nb // 2)), sb("scales%d" % (W2 + nb // 2))
+                    nb = nb % 2
                     nc.tensor.matmul_mx(
                         out=res[:, j, :], lhsT=w2c[:, nb * P:(nb + 1) * P].bitcast(FP8X4), lhsT_scale=w2s[:, nb * P:(nb + 1) * P],
                         rhs=sb("cc%d" % i0)[:].bitcast(FP8X4), rhs_scale=sb("cs%d" % i0)[:], start=True, stop=True)
@@ -169,47 +177,51 @@ def tile_moe_sdn_lin_gelu_kernel(tc, x_words, x_scales, w1, w2, gate, offs, pos1
                     nc.scalar.copy(out=stage[:], in_=res[:])
                 nc.sync.dma_start(out=out_v[:, part * per:(part + 1) * per, i0 * P:i1 * P], in_=stage[:])
 
-        for what in ["offs", "x0", 0, "xs", 1, "x1", 2, 3, 4, 5, 6, 7, "pos", 8, 9, 10, "gate"] + list(range(11, 25)):
+        for what in ["offs", "x0", 0, "xs", 1, "x1", 2, 3, 4, 5, 6, 7, "pos", 8, 9, 10, "g0", 11, "g1"] + list(range(12, 26)):
             load(what)
-        for e in range(E):
-            if e < 2:
-                gather_tokens(e)
+        gather_tokens(0)
+        gather_tokens(1)
         for i in range(10):
-            cast(i, "v" if i in (7, 9) else "s")
+            cast(i, "v" if i in (7, 9, 10) else "s")
             quantise(i)
             if i in (3, 5, 6):
-                gather_tokens({3: 2, 5: 3, 6: 4}[i])
+                gather_tokens((i + 2) // 2)
         for i in range(0, 10, 2):
             first_layer(i)
-        for i in range(10, 14):
-            cast(i, "s")
+        for i in range(10, 20):
+            cast(i, "v" if i in (7, 9, 10) else "s")
             quantise(i)
-        products(0, 0, 0, 5)
-        products(0, 1, 0, 5)
-        products(1, 0, 0, 5)
-        for i in range(14, 16):
-            cast(i, "s")
-            quantise(i)
-        products(1, 1, 0, 5)
-        for i in range(16, 24):
-            cast(i, "s" if i in (17, 19) else "v")
-            quantise(i)
-        for i in range(10, 24, 2):
-            first_layer(i)
         for b in range(2):
-            sums(b, 0, 3)
-            sums(b, 3, 5)
+            for r in range(2):
+                products(b, r, 0, 5)
+        for i in range(10, 16, 2):
+            first_layer(i, (0,))
+        for i in range(16, 20, 2):
+            first_layer(i)
+        for i in range(20, 24):
+            cast(i, "v" if i in (7, 9, 10) else "s")
+            quantise(i)
+        for i in range(10, 16, 2):
+            first_layer(i, (1,))
+        for i in range(20, 24, 2):
+            first_layer(i)
         products(2, 0, 0, 5)
         products(2, 1, 0, 5)
-        sums(2, 0, 3)
-        sums(2, 3, 5)
+        for b in range(2):
+            sums(b, 0, 3, "t%d" % (2 * b))
+            sums(b, 3, 5, "t%d" % (2 * b + 1))
         cast(24, "s")
         quantise(24)
-        groups = ((0, 2, "sv"), (2, 4, "sv"), (4, 5, "v"))
-        for i0, i1, eng in groups:
+        cast(25, "v")
+        quantise(25)
+        sums(2, 0, 3, "t0")
+        sums(2, 3, 5, "t1")
+
+        groups = ((0, 2, "sv"), (2, 4, "sv"), (4, 5, "vs"))
+        for g, (i0, i1, eng) in enumerate(groups):
             products(3, 0, i0, i1)
             products(3, 1, i0, i1)
-            sums(3, i0, i1)
-            turn(i0, i1)
+            sums(3, i0, i1, ("t2", "t0", "t2")[g])
+            turn(i0, i1, ("t3", "t1", "t3")[g])
             quant_c(i0, i1)
             second(i0, i1, eng)

from contextlib import ExitStack

import concourse.mybir as mybir
from concourse.masks import make_identity

K, T, E, C, H, N = 1024, 640, 5, 256, 512, 512
S = E * C
FLOPS = 2 * K * H * S + 2 * H * N * T

F32 = mybir.dt.float32
BF16 = mybir.dt.bfloat16
I32 = mybir.dt.int32
U32 = mybir.dt.uint32
U16 = mybir.dt.uint16
U8 = mybir.dt.uint8
FP8X4 = mybir.dt.float8_e4m3fn_x4
MULT = mybir.AluOpType.mult
GELU = mybir.ActivationFunctionType.Gelu_apprx_tanh

P = 128
PACK = 4
PASSES = K // (P * PACK)
BLOCKS = H // P
TILES = T // P


def tile_moe_sdn_lin_gelu_kernel(tc, x_words, x_scales, w1, w2, gate, offs, pos1, pos2, out):
    nc = tc.nc
    with ExitStack() as ctx:
        keep = ctx.enter_context(tc.tile_pool(name="keep", bufs=1))
        mxp = ctx.enter_context(tc.psum_pool(name="mxp", bufs=4))
        trp = ctx.enter_context(tc.psum_pool(name="trp", bufs=1))
        share = {"ct": "raw23", "h2": "raw19", "h3": "raw22", "prod1_0": "grp13", "prod1_1": "grp4", "prod2_1": "grp23", "grp24": "raw21", "grp25": "raw22", "gw1_2": "grp3", "gw1_3": "grp5", "h0": "raw5", "h1": "raw4", "stage0_0": "raw0", "stage0_1": "raw1", "stage2_0": "raw2", "stage2_1": "raw3", "stage4_0": "raw8", "stage4_1": "raw6", "grp20": "grp6", "grp21": "grp7", "grp22": "grp8", "grp16": "grp0", "grp17": "grp1", "grp18": "grp2", "grp19": "grp4"}
        made = {}
        where = {}

        def sb(name, shape=None, dtype=None):
            if name not in made:
                made[name] = keep.tile(shape, dtype, name=name, tag=share.get(name, name), align_bytes=64)
            return made[name]

        offs_t = keep.tile([P, S // 16], U16, name="offs_t")
        pos_t = [keep.tile([P, T // 16], U16, name="pos_t%d" % r) for r in range(2)]
        xw = [keep.tile([P, T], I32, name="xw%d" % s) for s in range(PASSES)]
        xs = keep.tile([P, T], U8, name="xs")
        gate_t = [keep.tile([P, T], F32, name="gate_t%d" % r) for r in range(2)]
        ident = keep.tile([P, P], F32, name="ident")
        warm = keep.tile([P, 8], F32, name="warm")
        warm2 = keep.tile([P, 8], F32, name="warm2")

        nc.vector.memset(xs[:].bitcast(I32), 0)
        nc.gpsimd.memset(warm[:], 0.0)
        nc.scalar.activation(warm2[:], warm[:], GELU)
        make_identity(nc, ident[:])

        chunks = [(e, s, 0, 256) for e in range(E) for s in range(PASSES)] + [(e, s, 256, 256) for e in range(3) for s in range(PASSES)] + [(e, s, c0, 128) for c0 in (256, 384) for e in range(3, E) for s in range(PASSES)]
        W2 = len(chunks)

        def load(what):
            if what == "offs":
                nc.sync.dma_start(offs_t[:], offs)
            elif what == "pos":
                nc.sync.dma_start(pos_t[0][:], pos1)
                nc.sync.dma_start(pos_t[1][:], pos2)
            elif what in ("x0", "x1"):
                s = 0 if what == "x0" else 1
                nc.sync.dma_start(out=xw[s][:], in_=x_words[s].rearrange("p t d -> p (t d)").bitcast(I32))
            elif what == "xs":
                for q in range(4):
                    nc.sync.dma_start(out=xs[32 * q:32 * q + 8, :].bitcast(I32), in_=x_scales[:, 4 * q:4 * q + 4, :].bitcast(I32))
            elif what in ("g0", "g1"):
                r = 0 if what == "g0" else 1
                nc.sync.dma_start(out=gate_t[r][:], in_=gate[r])
            else:
                if what >= W2:
                    rows = w2[:, (what - W2) * 256:(what - W2 + 1) * 256]
                else:
                    e, s, c0, width = chunks[what]
                    rows = w1[e, s * 512:(s + 1) * 512, c0:c0 + width]
                raw = sb("raw%d" % what, [P, PACK, rows.shape[1]], F32)
                nc.sync.dma_start(out=raw[:], in_=rows.rearrange("(p j) w -> p j w", j=PACK))

        def cast(i, engine):
            raw = sb("raw%d" % i)
            grouped = sb("grp%d" % i, [P, raw.shape[2] * PACK], BF16)
            dst = grouped[:].rearrange("p (c i t) -> p c t i", i=4, t=PACK)
            src = raw[:].rearrange("p t (c i) -> p c t i", i=4)
            if engine == "v":
                nc.vector.tensor_copy(out=dst, in_=src)
            elif engine == "g":
                nc.gpsimd.tensor_copy(out=dst, in_=src)
            else:
                nc.scalar.copy(out=dst, in_=src)

        def quantise(i):
            width = sb("raw%d" % i).shape[2]
            codes = sb("codes%d" % i, [P, width], U32)
            scales = sb("scales%d" % i, [P, width], U8)
            nc.vector.quantize_mx(out=codes[:].bitcast(FP8X4), scales=scales[:], in_=sb("grp%d" % i)[:])

        def gather_tokens(e):
            lst = offs_t[:, e * C // 16:(e + 1) * C // 16]
            nc.vector.tensor_copy(sb("gw0_%d" % e, [P, C], U32)[:], xw[0][:].bitcast(U32).indirect(lst))
            nc.vector.tensor_copy(sb("gw1_%d" % e, [P, C], U32)[:], xw[1][:].bitcast(U32).indirect(lst))
            nc.vector.tensor_copy(sb("gs_%d" % e, [P, C], U8)[:], xs[:].indirect(lst))

        def first_layer(i, only=None):
            e, s, c0, width = chunks[i]
            cols = slice(e * C, (e + 1) * C)
            for b0 in range(0, width, P):
                if only is not None and b0 // P not in only:
                    continue
                acc = mxp.tile([P, C], F32, name="acc", tag="mx")
                for s in range(PASSES):
                    nc.tensor.matmul_mx(
                        out=acc[:], lhsT=sb("codes%d" % (i + s))[:, b0:b0 + P].bitcast(FP8X4),
                        lhsT_scale=sb("scales%d" % (i + s))[:, b0:b0 + P],
                        rhs=sb("gw%d_%d" % (s, e))[:].bitcast(FP8X4), rhs_scale=sb("gs_%d" % e)[4 * s:P, :],
                        start=(s == 0), stop=(s == PASSES - 1))
                nc.scalar.activation(sb("h%d" % ((c0 + b0) // P), [P, S], F32)[:, cols], acc[:], GELU)

        def products(b, r, i0, i1):
            toks = slice(i0 * P, i1 * P)
            if b < 3:
                prod = sb("prod%d_%d" % (b, r), [P, T], F32)[:, toks]
            else:
                prod = sb("prodg%d" % i0, [P, 2, (i1 - i0) * P], F32)[:, r, :]
            for i in range(i0, i1):
                where[(b, r, i)] = prod[:, (i - i0) * P:(i - i0 + 1) * P]
            nc.vector.tensor_tensor(prod, sb("h%d" % b)[:].indirect(pos_t[r][:, i0 * 8:i1 * 8]), gate_t[r][:, toks], MULT)

        def sums(b, i0, i1, tag):
            ct4 = sb("ct", [P, TILES * H], BF16)[:].rearrange("p (i u q e) -> p i u q e", i=TILES, u=2, e=2)
            acc = trp.tile([P, i1 - i0, P], F32, name="sums", tag=tag)
            for i in range(i0, i1):
                for r in range(2):
                    nc.tensor.matmul(acc[:, i - i0, :], lhsT=where[(b, r, i)], rhs=ident[:],
                                     is_transpose=True, start=(r == 0), stop=(r == 1))
            nc.scalar.copy(out=ct4[:, i0:i1, :, 32 * b:32 * (b + 1), :],
                           in_=acc[:].rearrange("p i (m u e) -> p i u m e", u=2, e=2))

        out_v = out.rearrange("(nb p) t -> p nb t", p=P)

        def turn(i0, i1, tag):
            n = i1 - i0
            xt = trp.tile([P, n, 2, P], F32, name="xt", tag=tag)
            for i in range(i0, i1):
                words = sb("ct")[:, i * H:(i + 1) * H].bitcast(F32)
                for u in range(2):
                    nc.tensor.transpose(xt[:, i - i0, u, :], words[:, u * P:(u + 1) * P], ident[:])
            cg = sb("cg%d" % i0, [P, n * P * PACK], BF16)
            nc.scalar.copy(out=cg[:].bitcast(F32).rearrange("p (i r u) -> p i r u", u=2, i=n), in_=xt[:].rearrange("p i u r -> p i r u"))

        def quant_c(i0, i1):
            n = i1 - i0
            cc = sb("cc%d" % i0, [P, n * P], U32)
            cs = sb("cs%d" % i0, [P, n * P], U8)
            nc.vector.quantize_mx(out=cc[:].bitcast(FP8X4), scales=cs[:], in_=sb("cg%d" % i0)[:])

        def second(i0, i1, engines):
            n = i1 - i0
            n_parts = len(engines)
            per = N // P // n_parts
            for part in range(n_parts):
                res = mxp.tile([P, per, n * P], F32, name="res", tag="mx")
                for j in range(per):
                    nb = part * per + j
                    w2c, w2s = sb("codes%d" % (W2 + nb // 2)), sb("scales%d" % (W2 + nb // 2))
                    nb = nb % 2
                    nc.tensor.matmul_mx(
                        out=res[:, j, :], lhsT=w2c[:, nb * P:(nb + 1) * P].bitcast(FP8X4), lhsT_scale=w2s[:, nb * P:(nb + 1) * P],
                        rhs=sb("cc%d" % i0)[:].bitcast(FP8X4), rhs_scale=sb("cs%d" % i0)[:], start=True, stop=True)
                stage = sb("stage%d_%d" % (i0, part), [P, per, n * P], F32)
                if engines[part] == "v":
                    nc.vector.tensor_copy(out=stage[:], in_=res[:])
                else:
                    nc.scalar.copy(out=stage[:], in_=res[:])
                nc.sync.dma_start(out=out_v[:, part * per:(part + 1) * per, i0 * P:i1 * P], in_=stage[:])

        for what in ["offs", "x0", 0, "xs", 1, "x1", 2, 3, 4, 5, 6, 7, "pos", 8, 9, 10, "g0", 11, "g1"] + list(range(12, 26)):
            load(what)
        gather_tokens(0)
        gather_tokens(1)
        for i in range(10):
            cast(i, "v" if i in (7, 9, 10) else "s")
            quantise(i)
            if i in (3, 5, 6):
                gather_tokens((i + 2) // 2)
        for i in range(0, 10, 2):
            first_layer(i)
        for i in range(10, 20):
            cast(i, "v" if i in (7, 9, 10) else "s")
            quantise(i)
        for b in range(2):
            for r in range(2):
                products(b, r, 0, 5)
        for i in range(10, 16, 2):
            first_layer(i, (0,))
        for i in range(16, 20, 2):
            first_layer(i)
        for i in range(20, 24):
            cast(i, "v" if i in (7, 9, 10) else "s")
            quantise(i)
        for i in range(10, 16, 2):
            first_layer(i, (1,))
        for i in range(20, 24, 2):
            first_layer(i)
        products(2, 0, 0, 5)
        products(2, 1, 0, 5)
        for b in range(2):
            sums(b, 0, 3, "t%d" % (2 * b))
            sums(b, 3, 5, "t%d" % (2 * b + 1))
        cast(24, "s")
        quantise(24)
        cast(25, "v")
        quantise(25)
        sums(2, 0, 3, "t0")
        sums(2, 3, 5, "t1")

        groups = ((0, 2, "sv"), (2, 4, "sv"), (4, 5, "vs"))
        for g, (i0, i1, eng) in enumerate(groups):
            products(3, 0, i0, i1)
            products(3, 1, i0, i1)
            sums(3, i0, i1, ("t2", "t0", "t2")[g])
            turn(i0, i1, ("t3", "t1", "t3")[g])
            quant_c(i0, i1)
            second(i0, i1, eng)
